import numpy as np
import ml_dtypes


def mxq(x, axis, fmt="e4m3"):
    dtype, down = {"e4m3": (ml_dtypes.float8_e4m3fn, 7), "e5m2": (ml_dtypes.float8_e5m2, 14)}[fmt]
    v = np.moveaxis(np.asarray(x, np.float32).astype(ml_dtypes.bfloat16).astype(np.float64), axis, -1)
    blocks = v.reshape(v.shape[:-1] + (-1, 32))
    amax = np.abs(blocks).max(-1, keepdims=True)
    byte = np.maximum(np.where(amax > 0, np.frexp(amax)[1] - 1 + 127, 0) - down, 1)
    scale = np.exp2(byte - 127.0)
    codes = (blocks / scale).astype(np.float32).astype(dtype).astype(np.float64)
    return np.moveaxis((codes * scale).reshape(v.shape), -1, axis)


WIDE = False


def mx_kscale(k):
    if not WIDE:
        return np.ones(k)
    levels = np.array([30, -30])
    if k % 512:
        return np.exp2(np.random.permutation(np.resize(levels, k // 32))).repeat(32)
    a = np.empty((k // 512, 16))
    for p in range(k // 512):
        a[p, :8] = np.random.permutation(np.resize(levels, 8))
        for g in range(8):
            far = levels[np.abs(levels - a[p, g]) >= 10]
            a[p, g + 8] = far[np.random.randint(len(far))]
    return np.exp2(a.ravel()).repeat(32)


def f64(x):
    return np.asarray(x).astype(np.float64)


def striped(idx):
    return np.tile(np.asarray(idx).reshape(-1, 16).T, (8, 1)).astype(np.uint16)


def unstriped(offs):
    return offs[:16].T.reshape(-1).astype(np.int64)


E2M1 = np.array([0.0, 0.5, 1.0, 1.5, 2.0, 3.0, 4.0, 6.0, -0.0, -0.5, -1.0, -1.5, -2.0, -3.0, -4.0, -6.0])


def pack_weight(w, fmt):
    k, n = w.shape
    w = f64(np.asarray(w, np.float32).astype(ml_dtypes.bfloat16)).reshape(k // 32, 32, n)
    amax = np.abs(w).max(1)
    if fmt in ("e4m3", "e5m2"):
        byte = np.frexp(amax)[1] - 1 + 127 - (7 if fmt == "e4m3" else 14)
    else:
        mant, ex = np.frexp(amax / 6.0)
        byte = np.where(mant > 0.5, ex, ex - 1) + 127
    byte = np.clip(np.where(amax > 0, byte, 1), 1, 254)
    scaled = (w * np.exp2(127.0 - byte)[:, None, :]).reshape(k, n).astype(np.float32)
    by_word = np.ascontiguousarray(scaled.reshape(k // 512, 128, 4, n).transpose(0, 1, 3, 2))
    if fmt in ("e4m3", "e5m2"):
        words = by_word.astype(ml_dtypes.float8_e4m3fn if fmt == "e4m3" else ml_dtypes.float8_e5m2).view(np.uint8)
    else:
        c = by_word.astype(ml_dtypes.float4_e2m1fn).view(np.uint8) & 0xF
        words = (c[..., 0::2] | (c[..., 1::2] << 4)).reshape(k // 512, 128, 2 * n)
    return np.ascontiguousarray(words), np.ascontiguousarray(byte.astype(np.uint8).reshape(k // 512, 16, n))


def unpack_weight(words, scales, fmt):
    g, _, n = scales.shape
    words = np.ascontiguousarray(words).reshape(g, 128, n, -1)
    if fmt in ("e4m3", "e5m2"):
        vals = words.view(ml_dtypes.float8_e4m3fn if fmt == "e4m3" else ml_dtypes.float8_e5m2).astype(np.float64)
    else:
        nib = np.empty((g, 128, n, 4), np.uint8)
        nib[..., 0::2] = words & 0xF
        nib[..., 1::2] = words >> 4
        vals = E2M1[nib]
    vals = vals * np.repeat(np.exp2(scales.astype(np.float64) - 127.0), 8, axis=1)[..., None]
    return vals.transpose(0, 1, 3, 2).reshape(g * 512, n)


K, T, J, R, V, N = 512, 2048, 256, 512, 512, 256


def setup_inputs():
    n = np.random.standard_normal
    idx = np.random.permutation(T)[:J]
    idx2 = np.random.permutation(T)[:J]
    idx3 = np.random.permutation(V)[:J]
    idx4 = np.random.permutation(V)[:J]
    fk = mx_kscale(K)
    fr = mx_kscale(R)
    xtp = pack_weight(n((K, T)) / fk[:, None], "e4m3")
    wp = pack_weight(n((K, R)) * 1 / np.sqrt(K) * fk[:, None] * fr, "e2m1")
    wbp = pack_weight(n((R, N)) * 1 / np.sqrt(R) / fr[:, None], "e5m2")
    return {
        "xt_words": xtp[0],
        "xt_scales": xtp[1],
        "w_words": wp[0],
        "w_scales": wp[1],
        "tb": (n((R, V))).astype(np.float32),
        "wb_words": wbp[0],
        "wb_scales": wbp[1],
        "offs": striped(idx),
        "offs2": striped(idx2),
        "offs3": striped(idx3),
        "offs4": striped(idx4),
    }


def reference(xt_words, xt_scales, w_words, w_scales, tb, wb_words, wb_scales, offs, offs2, offs3, offs4):
    idx = unstriped(offs)
    idx2 = unstriped(offs2)
    idx3 = unstriped(offs3)
    idx4 = unstriped(offs4)
    xtu = unpack_weight(xt_words, xt_scales, "e4m3")
    wu = unpack_weight(w_words, w_scales, "e2m1")
    wbu = unpack_weight(wb_words, wb_scales, "e5m2")
    xtidxg = xtu[:, idx]
    a = wu.T @ xtidxg
    xtidx2g = xtu[:, idx2]
    da = wu.T @ xtidx2g
    hid = a * f64(tb)[:, idx3]
    dh = da * f64(tb)[:, idx3] + a * f64(tb)[:, idx4]
    hidq = mxq(hid, 0, "e4m3")
    p = wbu.T @ hidq
    dhq = mxq(dh, 0, "e5m2")
    dp = wbu.T @ dhq
    y = p + 0.5 * dp
    return y

@@ -1,0 +1,170 @@
+from contextlib import ExitStack
+
+import concourse.mybir as mybir
+
+K, T, J, R, V, N = 512, 2048, 256, 512, 512, 256
+FLOPS = 2 * (2 * K * R * J + 2 * R * N * J)
+
+F32 = mybir.dt.float32
+BF16 = mybir.dt.bfloat16
+I32 = mybir.dt.int32
+U32 = mybir.dt.uint32
+U16 = mybir.dt.uint16
+U8 = mybir.dt.uint8
+E4M3X4 = mybir.dt.float8_e4m3fn_x4
+E5M2X4 = mybir.dt.float8_e5m2_x4
+E2M1X4 = mybir.dt.float4_e2m1fn_x4
+MULT = mybir.AluOpType.mult
+ADD = mybir.AluOpType.add
+COPY = mybir.ActivationFunctionType.Copy
+
+P = 128
+PACK = 4
+HALVES = 2
+JH = J // HALVES
+RUN = 4
+
+
+def load_scale_rows(queues, plane, scales):
+    for q, queue in enumerate(queues):
+        queue.dma_start(out=plane[32 * q : 32 * q + 4, :].bitcast(I32), in_=scales[0, 4 * q : 4 * q + 4, :].bitcast(I32))
+
+
+def by_runs(slabs):
+    return slabs.rearrange("p t (c i) -> p c t i", i=RUN)
+
+
+def woven_by_runs(woven):
+    return woven.rearrange("p (c i) t -> p c t i", i=RUN)
+
+
+def tile_list_firstorder_two_moved_kernel(
+    tc, xt_words, xt_scales, w_words, w_scales, tb, wb_words, wb_scales, offs, offs2, offs3, offs4, out
+):
+    nc = tc.nc
+    with ExitStack() as ctx:
+        keep = ctx.enter_context(tc.tile_pool(name="keep", bufs=1))
+        psum = ctx.enter_context(tc.psum_pool(name="psum", bufs=1))
+
+        def sb(name, shape, dtype, tag=None):
+            return keep.tile(shape, dtype, name=name, tag=tag or name, align_bytes=64)
+
+        lists = [keep.tile([P, J // 16], U16, name="list%d" % i) for i in range(4)]
+        x_table = sb("x_table", [P, T], I32)
+        x_plane = sb("x_plane", [P, T], U8, tag="x_plane_then_wb")
+        w_raw = sb("w_raw", [P, 2 * R], U8)
+        weight_plane = sb("weight_plane", [P, R], U8)
+        tb_rows = [sb("tb_rows%d" % t, [P, V], F32) for t in range(PACK)]
+
+        nc.vector.memset(x_plane[:, : T // 2].bitcast(I32), 0)
+        nc.gpsimd.memset(x_plane[:, T // 2 :].bitcast(I32), 0)
+        nc.vector.memset(weight_plane[:].bitcast(I32), 0)
+
+        tb_dealt = tb.rearrange("(p t) v -> p t v", t=PACK)
+        nc.sync.dma_start(lists[0][:], offs)
+        nc.sync.dma_start(lists[1][:], offs2)
+        nc.sync.dma_start(out=w_raw[:].bitcast(I32), in_=w_words[0].bitcast(I32))
+        load_scale_rows([nc.sync] * 4, x_plane, xt_scales)
+        nc.sync.dma_start(out=x_table[:], in_=xt_words[0].rearrange("p n t -> p (n t)").bitcast(I32))
+        load_scale_rows([nc.sync] * 4, weight_plane, w_scales)
+        nc.sync.dma_start(lists[2][:], offs3)
+        for t in range(PACK):
+            nc.sync.dma_start(out=tb_rows[t][:], in_=tb_dealt[:, t, :])
+            if t == 1:
+                nc.sync.dma_start(lists[3][:], offs4)
+
+        w_codes = sb("w_codes", [P, PACK, 2 * P], U8)
+        w_plane = sb("w_plane", [P, PACK, P], U8)
+        nc.vector.tensor_copy(out=w_codes[:].bitcast(U16), in_=w_raw[:].bitcast(U16).rearrange("p (m t) -> p t m", t=PACK))
+
+        x_codes = sb("x_codes", [P, 2, J], U32)
+        x_scales = sb("x_scales", [P, 2, J], U8)
+        for i in range(2):
+            nc.vector.tensor_copy(x_scales[:, i, :], x_plane[:].indirect(lists[i][:]))
+        nc.vector.tensor_copy(out=w_plane[:], in_=weight_plane[:].rearrange("p (m t) -> p t m", t=PACK))
+        for i in range(2):
+            nc.vector.tensor_copy(x_codes[:, i, :], x_table[:].bitcast(U32).indirect(lists[i][:]))
+
+        wb_codes = sb("wb_codes", [P, N], I32, tag="x_plane_then_wb")
+        nc.sync.dma_start(out=wb_codes[:], in_=wb_words[0].rearrange("p n t -> p (n t)").bitcast(I32))
+        wb_plane = weight_plane[:, 0:N]
+        load_scale_rows([nc.sync] * 4, wb_plane, wb_scales)
+
+        entry = sb("entry", [P, PACK, J], F32)
+        d_entry = sb("d_entry", [P, PACK, J], F32)
+        by_entry = sb("by_entry", [P, PACK, 2, J], F32)
+        entry_term = sb("entry_term", [P, PACK, J], F32)
+        for t in range(PACK):
+            bank = psum.tile([P, 2, J], F32, name="first_bank%d" % t)
+            nc.tensor.matmul_mx(
+                out=bank[:].rearrange("p s j -> p (s j)"),
+                lhsT=w_codes[:, t, :].bitcast(E2M1X4),
+                lhsT_scale=w_plane[:, t, :],
+                rhs=x_codes[:].rearrange("p s j -> p (s j)").bitcast(E4M3X4),
+                rhs_scale=x_scales[:].rearrange("p s j -> p (s j)"),
+                start=True,
+                stop=True,
+            )
+            nc.scalar.activation(entry[:, t, :], tb_rows[t][:].indirect(lists[2][:]), COPY)
+            if t == 0:
+                nc.vector.tensor_copy(d_entry[:, t, :], tb_rows[t][:].indirect(lists[3][:]))
+            else:
+                nc.scalar.activation(d_entry[:, t, :], tb_rows[t][:].indirect(lists[3][:]), COPY)
+            nc.vector.scalar_tensor_tensor(
+                out=by_entry[:, t, :, :],
+                in0=bank[:],
+                scalar=0.5,
+                in1=entry[:, t : t + 1, :].to_broadcast([P, 2, J]),
+                op0=MULT,
+                op1=MULT,
+            )
+            nc.vector.scalar_tensor_tensor(
+                out=entry_term[:, t, :], in0=bank[:, 0, :], scalar=0.5, in1=d_entry[:, t, :], op0=MULT, op1=MULT
+            )
+
+        out_rows = out.rearrange("(u p) j -> p u j", p=P)
+        for h in range(HALVES):
+            cols = slice(h * JH, (h + 1) * JH)
+            hid = sb("hid%d" % h, [P, JH, PACK], BF16)
+            dh = sb("dh%d" % h, [P, JH, PACK], BF16)
+            hid_codes = sb("hid_codes%d" % h, [P, JH], U32)
+            hid_scales = sb("hid_scales%d" % h, [P, JH], U8)
+            dh_codes = sb("dh_codes%d" % h, [P, JH], U32)
+            dh_scales = sb("dh_scales%d" % h, [P, JH], U8)
+            nc.scalar.activation(woven_by_runs(hid[:]), by_runs(by_entry[:, :, 0, cols]), COPY, scale=2.0)
+            nc.vector.tensor_tensor(
+                out=woven_by_runs(dh[:]), in0=by_runs(by_entry[:, :, 1, cols]), in1=by_runs(entry_term[:, :, cols]), op=ADD
+            )
+            nc.vector.quantize_mx(
+                out=hid_codes[:].bitcast(E4M3X4), scales=hid_scales[:], in_=hid[:].rearrange("p j t -> p (j t)")
+            )
+            nc.vector.quantize_mx(
+                out=dh_codes[:].bitcast(E5M2X4), scales=dh_scales[:], in_=dh[:].rearrange("p j t -> p (j t)")
+            )
+            result = sb("result%d" % h, [P, N // P, JH], F32)
+            for u in range(N // P):
+                feats = slice(u * P, (u + 1) * P)
+                bank = psum.tile([P, JH], F32, name="out_bank%d_%d" % (h, u))
+                nc.tensor.matmul_mx(
+                    out=bank[:],
+                    lhsT=wb_codes[:, feats].bitcast(E5M2X4),
+                    lhsT_scale=wb_plane[:, feats],
+                    rhs=hid_codes[:].bitcast(E4M3X4),
+                    rhs_scale=hid_scales[:],
+                    start=True,
+                    stop=False,
+                )
+                nc.tensor.matmul_mx(
+                    out=bank[:],
+                    lhsT=wb_codes[:, feats].bitcast(E5M2X4),
+                    lhsT_scale=wb_plane[:, feats],
+                    rhs=dh_codes[:].bitcast(E5M2X4),
+                    rhs_scale=dh_scales[:],
+                    start=False,
+                    stop=True,
+                )
+                if h == HALVES - 1 and u == 1:
+                    nc.vector.tensor_copy(out=result[:, u, :], in_=bank[:])
+                else:
+                    nc.scalar.copy(out=result[:, u, :], in_=bank[:])
+            nc.sync.dma_start(out=out_rows[:, :, cols], in_=result[:])

@@ -54,24 +54,28 @@ def tile_list_firstorder_two_moved_kernel(
         x_plane = sb("x_plane", [P, T], U8, tag="x_plane_then_wb")
         w_raw = sb("w_raw", [P, 2 * R], U8)
         weight_plane = sb("weight_plane", [P, R], U8)
-        tb_rows = [sb("tb_rows%d" % t, [P, V], F32) for t in range(PACK)]
+        tb_rows = [sb("tb_rows%d" % g, [P, 2, V], F32) for g in range(2)]
 
         nc.vector.memset(x_plane[:, : T // 2].bitcast(I32), 0)
         nc.gpsimd.memset(x_plane[:, T // 2 :].bitcast(I32), 0)
         nc.vector.memset(weight_plane[:].bitcast(I32), 0)
 
+        warm = sb("warm", [P, 16], F32)
+        nc.vector.memset(warm[:, 0:1], 0.0)
+
         tb_dealt = tb.rearrange("(p t) v -> p t v", t=PACK)
         nc.sync.dma_start(lists[0][:], offs)
         nc.sync.dma_start(lists[1][:], offs2)
         nc.sync.dma_start(out=w_raw[:].bitcast(I32), in_=w_words[0].bitcast(I32))
-        load_scale_rows([nc.sync] * 4, x_plane, xt_scales)
+        load_scale_rows([nc.sync, nc.scalar] * 2, x_plane, xt_scales)
         nc.sync.dma_start(out=x_table[:], in_=xt_words[0].rearrange("p n t -> p (n t)").bitcast(I32))
         load_scale_rows([nc.sync] * 4, weight_plane, w_scales)
         nc.sync.dma_start(lists[2][:], offs3)
-        for t in range(PACK):
-            nc.sync.dma_start(out=tb_rows[t][:], in_=tb_dealt[:, t, :])
-            if t == 1:
-                nc.sync.dma_start(lists[3][:], offs4)
+        nc.sync.dma_start(lists[3][:], offs4)
+        for g in range(2):
+            nc.sync.dma_start(out=tb_rows[g][:], in_=tb_dealt[:, 2 * g : 2 * g + 2, :])
+
+        nc.scalar.activation(warm[:, 8:9], warm[:, 0:1], COPY)
 
         w_codes = sb("w_codes", [P, PACK, 2 * P], U8)
         w_plane = sb("w_plane", [P, PACK, P], U8)
@@ -81,90 +85,102 @@ def tile_list_firstorder_two_moved_kernel(
         x_scales = sb("x_scales", [P, 2, J], U8)
         for i in range(2):
             nc.vector.tensor_copy(x_scales[:, i, :], x_plane[:].indirect(lists[i][:]))
+        nc.vector.tensor_copy(x_codes[:, 0, :], x_table[:].bitcast(U32).indirect(lists[0][:]))
         nc.vector.tensor_copy(out=w_plane[:], in_=weight_plane[:].rearrange("p (m t) -> p t m", t=PACK))
-        for i in range(2):
-            nc.vector.tensor_copy(x_codes[:, i, :], x_table[:].bitcast(U32).indirect(lists[i][:]))
+        nc.vector.tensor_copy(x_codes[:, 1, :], x_table[:].bitcast(U32).indirect(lists[1][:]))
 
         wb_codes = sb("wb_codes", [P, N], I32, tag="x_plane_then_wb")
         nc.sync.dma_start(out=wb_codes[:], in_=wb_words[0].rearrange("p n t -> p (n t)").bitcast(I32))
         wb_plane = weight_plane[:, 0:N]
         load_scale_rows([nc.sync] * 4, wb_plane, wb_scales)
 
+        banks = [[psum.tile([P, 2, J], F32, name="first_bank%d_%d" % (i, g)) for g in range(2)] for i in range(2)]
+        for g in range(2):
+            for i in range(2):
+                for t in (2 * g, 2 * g + 1):
+                    nc.tensor.matmul_mx(
+                        out=banks[i][g][:, t % 2, :],
+                        lhsT=w_codes[:, t, :].bitcast(E2M1X4),
+                        lhsT_scale=w_plane[:, t, :],
+                        rhs=x_codes[:, i, :].bitcast(E4M3X4),
+                        rhs_scale=x_scales[:, i, :],
+                        start=True,
+                        stop=True,
+                    )
+
         entry = sb("entry", [P, PACK, J], F32)
         d_entry = sb("d_entry", [P, PACK, J], F32)
-        by_entry = sb("by_entry", [P, PACK, 2, J], F32)
+        hid_slabs = sb("hid_slabs", [P, PACK, J], F32)
+        token_term = sb("token_term", [P, PACK, J], F32)
         entry_term = sb("entry_term", [P, PACK, J], F32)
-        for t in range(PACK):
-            bank = psum.tile([P, 2, J], F32, name="first_bank%d" % t)
-            nc.tensor.matmul_mx(
-                out=bank[:].rearrange("p s j -> p (s j)"),
-                lhsT=w_codes[:, t, :].bitcast(E2M1X4),
-                lhsT_scale=w_plane[:, t, :],
-                rhs=x_codes[:].rearrange("p s j -> p (s j)").bitcast(E4M3X4),
-                rhs_scale=x_scales[:].rearrange("p s j -> p (s j)"),
-                start=True,
-                stop=True,
-            )
-            nc.scalar.activation(entry[:, t, :], tb_rows[t][:].indirect(lists[2][:]), COPY)
-            if t == 0:
-                nc.vector.tensor_copy(d_entry[:, t, :], tb_rows[t][:].indirect(lists[3][:]))
-            else:
-                nc.scalar.activation(d_entry[:, t, :], tb_rows[t][:].indirect(lists[3][:]), COPY)
+        for g in range(2):
+            pair = slice(2 * g, 2 * g + 2)
+            for t in (2 * g, 2 * g + 1):
+                if t == 1:
+                    nc.vector.tensor_copy(entry[:, t, :], tb_rows[g][:, t % 2, :].indirect(lists[2][:]))
+                else:
+                    nc.scalar.activation(entry[:, t, :], tb_rows[g][:, t % 2, :].indirect(lists[2][:]), COPY)
+            for t in (2 * g, 2 * g + 1):
+                nc.scalar.activation(d_entry[:, t, :], tb_rows[g][:, t % 2, :].indirect(lists[3][:]), COPY)
+            nc.vector.tensor_tensor(out=hid_slabs[:, pair, :], in0=banks[0][g][:], in1=entry[:, pair, :], op=MULT)
             nc.vector.scalar_tensor_tensor(
-                out=by_entry[:, t, :, :],
-                in0=bank[:],
-                scalar=0.5,
-                in1=entry[:, t : t + 1, :].to_broadcast([P, 2, J]),
-                op0=MULT,
-                op1=MULT,
+                out=token_term[:, pair, :], in0=banks[1][g][:], scalar=0.5, in1=entry[:, pair, :], op0=MULT, op1=MULT
             )
             nc.vector.scalar_tensor_tensor(
-                out=entry_term[:, t, :], in0=bank[:, 0, :], scalar=0.5, in1=d_entry[:, t, :], op0=MULT, op1=MULT
+                out=entry_term[:, pair, :], in0=banks[0][g][:], scalar=0.5, in1=d_entry[:, pair, :], op0=MULT, op1=MULT
+            )
+
+        halves = [slice(h * JH, (h + 1) * JH) for h in range(HALVES)]
+        hid = sb("hid", [P, J, PACK], BF16)
+        hid_codes = sb("hid_codes", [P, J], U32)
+        hid_scales = sb("hid_scales", [P, J], U8)
+        dh = [sb("dh%d" % h, [P, JH, PACK], BF16) for h in range(HALVES)]
+        dh_codes = [sb("dh_codes%d" % h, [P, JH], U32) for h in range(HALVES)]
+        dh_scales = [sb("dh_scales%d" % h, [P, JH], U8) for h in range(HALVES)]
+
+        def join_terms(h):
+            nc.vector.tensor_tensor(
+                out=woven_by_runs(dh[h][:]),
+                in0=by_runs(token_term[:, :, halves[h]]),
+                in1=by_runs(entry_term[:, :, halves[h]]),
+                op=ADD,
+            )
+
+        nc.scalar.copy(out=woven_by_runs(hid[:]), in_=by_runs(hid_slabs[:]))
+        join_terms(0)
+        nc.vector.quantize_mx(
+            out=hid_codes[:].bitcast(E4M3X4), scales=hid_scales[:], in_=hid[:].rearrange("p j t -> p (j t)")
+        )
+        join_terms(1)
+        for h in range(HALVES):
+            nc.vector.quantize_mx(
+                out=dh_codes[h][:].bitcast(E5M2X4), scales=dh_scales[h][:], in_=dh[h][:].rearrange("p j t -> p (j t)")
             )
 
         out_rows = out.rearrange("(u p) j -> p u j", p=P)
+        out_banks = [[psum.tile([P, JH], F32, name="out_bank%d_%d" % (h, u)) for u in range(N // P)] for h in range(HALVES)]
+
+        def second_pass(h, u, codes, scales, first):
+            feats = slice(u * P, (u + 1) * P)
+            nc.tensor.matmul_mx(
+                out=out_banks[h][u][:],
+                lhsT=wb_codes[:, feats].bitcast(E5M2X4),
+                lhsT_scale=wb_plane[:, feats],
+                rhs=codes,
+                rhs_scale=scales,
+                start=first,
+                stop=not first,
+            )
+
         for h in range(HALVES):
-            cols = slice(h * JH, (h + 1) * JH)
-            hid = sb("hid%d" % h, [P, JH, PACK], BF16)
-            dh = sb("dh%d" % h, [P, JH, PACK], BF16)
-            hid_codes = sb("hid_codes%d" % h, [P, JH], U32)
-            hid_scales = sb("hid_scales%d" % h, [P, JH], U8)
-            dh_codes = sb("dh_codes%d" % h, [P, JH], U32)
-            dh_scales = sb("dh_scales%d" % h, [P, JH], U8)
-            nc.scalar.activation(woven_by_runs(hid[:]), by_runs(by_entry[:, :, 0, cols]), COPY, scale=2.0)
-            nc.vector.tensor_tensor(
-                out=woven_by_runs(dh[:]), in0=by_runs(by_entry[:, :, 1, cols]), in1=by_runs(entry_term[:, :, cols]), op=ADD
-            )
-            nc.vector.quantize_mx(
-                out=hid_codes[:].bitcast(E4M3X4), scales=hid_scales[:], in_=hid[:].rearrange("p j t -> p (j t)")
-            )
-            nc.vector.quantize_mx(
-                out=dh_codes[:].bitcast(E5M2X4), scales=dh_scales[:], in_=dh[:].rearrange("p j t -> p (j t)")
-            )
+            for u in range(N // P):
+                second_pass(h, u, hid_codes[:, halves[h]].bitcast(E4M3X4), hid_scales[:, halves[h]], True)
+        for h in range(HALVES):
             result = sb("result%d" % h, [P, N // P, JH], F32)
             for u in range(N // P):
-                feats = slice(u * P, (u + 1) * P)
-                bank = psum.tile([P, JH], F32, name="out_bank%d_%d" % (h, u))
-                nc.tensor.matmul_mx(
-                    out=bank[:],
-                    lhsT=wb_codes[:, feats].bitcast(E5M2X4),
-                    lhsT_scale=wb_plane[:, feats],
-                    rhs=hid_codes[:].bitcast(E4M3X4),
-                    rhs_scale=hid_scales[:],
-                    start=True,
-                    stop=False,
-                )
-                nc.tensor.matmul_mx(
-                    out=bank[:],
-                    lhsT=wb_codes[:, feats].bitcast(E5M2X4),
-                    lhsT_scale=wb_plane[:, feats],
-                    rhs=dh_codes[:].bitcast(E5M2X4),
-                    rhs_scale=dh_scales[:],
-                    start=False,
-                    stop=True,
-                )
-                if h == HALVES - 1 and u == 1:
-                    nc.vector.tensor_copy(out=result[:, u, :], in_=bank[:])
+                second_pass(h, u, dh_codes[h][:].bitcast(E5M2X4), dh_scales[h][:], False)
+                if u == 1:
+                    nc.vector.tensor_copy(out=result[:, u, :], in_=out_banks[h][u][:])
                 else:
-                    nc.scalar.copy(out=result[:, u, :], in_=bank[:])
-            nc.sync.dma_start(out=out_rows[:, :, cols], in_=result[:])
+                    nc.scalar.copy(out=result[:, u, :], in_=out_banks[h][u][:])
+            nc.sync.dma_start(out=out_rows[:, :, halves[h]], in_=result[:])

@@ -53,12 +53,16 @@ def tile_list_firstorder_two_moved_kernel(
         x_table = sb("x_table", [P, T], I32)
         x_plane = sb("x_plane", [P, T], U8, tag="x_plane_then_wb")
         w_raw = sb("w_raw", [P, 2 * R], U8)
-        weight_plane = sb("weight_plane", [P, R], U8)
-        tb_rows = [sb("tb_rows%d" % g, [P, 2, V], F32) for g in range(2)]
+        w_raw_plane = sb("w_raw_plane", [P, R], U8, tag="w_plane_then_codes")
+        wb_plane = sb("wb_plane", [P, N], U8)
+        tb_low = sb("tb_low", [P, 2, V], F32)
+        tb_high = [sb("tb_high%d" % t, [P, V], F32) for t in range(2)]
+        tb_rows = [tb_low[:, 0, :], tb_low[:, 1, :], tb_high[0][:], tb_high[1][:]]
 
         nc.vector.memset(x_plane[:, : T // 2].bitcast(I32), 0)
         nc.gpsimd.memset(x_plane[:, T // 2 :].bitcast(I32), 0)
-        nc.vector.memset(weight_plane[:].bitcast(I32), 0)
+        nc.vector.memset(w_raw_plane[:].bitcast(I32), 0)
+        nc.vector.memset(wb_plane[:].bitcast(I32), 0)
 
         warm = sb("warm", [P, 16], F32)
         nc.vector.memset(warm[:, 0:1], 0.0)
@@ -69,11 +73,12 @@ def tile_list_firstorder_two_moved_kernel(
         nc.sync.dma_start(out=w_raw[:].bitcast(I32), in_=w_words[0].bitcast(I32))
         load_scale_rows([nc.sync, nc.scalar] * 2, x_plane, xt_scales)
         nc.sync.dma_start(out=x_table[:], in_=xt_words[0].rearrange("p n t -> p (n t)").bitcast(I32))
-        load_scale_rows([nc.sync] * 4, weight_plane, w_scales)
+        load_scale_rows([nc.sync] * 4, w_raw_plane, w_scales)
+        nc.sync.dma_start(out=tb_low[:], in_=tb_dealt[:, 0:2, :])
         nc.sync.dma_start(lists[2][:], offs3)
         nc.sync.dma_start(lists[3][:], offs4)
-        for g in range(2):
-            nc.sync.dma_start(out=tb_rows[g][:], in_=tb_dealt[:, 2 * g : 2 * g + 2, :])
+        for t in (2, 3):
+            nc.sync.dma_start(out=tb_rows[t], in_=tb_dealt[:, t, :])
 
         nc.scalar.activation(warm[:, 8:9], warm[:, 0:1], COPY)
 
@@ -81,59 +86,65 @@ def tile_list_firstorder_two_moved_kernel(
         w_plane = sb("w_plane", [P, PACK, P], U8)
         nc.vector.tensor_copy(out=w_codes[:].bitcast(U16), in_=w_raw[:].bitcast(U16).rearrange("p (m t) -> p t m", t=PACK))
 
-        x_codes = sb("x_codes", [P, 2, J], U32)
-        x_scales = sb("x_scales", [P, 2, J], U8)
+        x_scales = [sb("x_scales%d" % i, [P, J], U8) for i in range(2)]
         for i in range(2):
-            nc.vector.tensor_copy(x_scales[:, i, :], x_plane[:].indirect(lists[i][:]))
-        nc.vector.tensor_copy(x_codes[:, 0, :], x_table[:].bitcast(U32).indirect(lists[0][:]))
-        nc.vector.tensor_copy(out=w_plane[:], in_=weight_plane[:].rearrange("p (m t) -> p t m", t=PACK))
-        nc.vector.tensor_copy(x_codes[:, 1, :], x_table[:].bitcast(U32).indirect(lists[1][:]))
+            nc.vector.tensor_copy(x_scales[i][:], x_plane[:].indirect(lists[i][:]))
+        token_codes = sb("token_codes", [P, J], U32)
+        nc.vector.tensor_copy(token_codes[:], x_table[:].bitcast(U32).indirect(lists[0][:]))
+        nc.vector.tensor_copy(out=w_plane[:], in_=w_raw_plane[:].rearrange("p (m t) -> p t m", t=PACK))
+        change_codes = sb("change_codes", [P, J], U32, tag="w_plane_then_codes")
+        nc.vector.tensor_copy(change_codes[:], x_table[:].bitcast(U32).indirect(lists[1][:]))
+        x_codes = [token_codes, change_codes]
 
         wb_codes = sb("wb_codes", [P, N], I32, tag="x_plane_then_wb")
         nc.sync.dma_start(out=wb_codes[:], in_=wb_words[0].rearrange("p n t -> p (n t)").bitcast(I32))
-        wb_plane = weight_plane[:, 0:N]
         load_scale_rows([nc.sync] * 4, wb_plane, wb_scales)
 
-        banks = [[psum.tile([P, 2, J], F32, name="first_bank%d_%d" % (i, g)) for g in range(2)] for i in range(2)]
-        for g in range(2):
+        def first_pass(bank_cols, t, codes, scales):
+            nc.tensor.matmul_mx(
+                out=bank_cols,
+                lhsT=w_codes[:, t, :].bitcast(E2M1X4),
+                lhsT_scale=w_plane[:, t, :],
+                rhs=codes.bitcast(E4M3X4),
+                rhs_scale=scales,
+                start=True,
+                stop=True,
+            )
+
+        low_banks = [psum.tile([P, 2, J], F32, name="low_bank%d" % i) for i in range(2)]
+        high_banks = [psum.tile([P, 2, J], F32, name="high_bank%d" % t) for t in range(2)]
+        for i in range(2):
+            for t in (0, 1):
+                first_pass(low_banks[i][:, t, :], t, x_codes[i][:], x_scales[i][:])
+        for t in (2, 3):
             for i in range(2):
-                for t in (2 * g, 2 * g + 1):
-                    nc.tensor.matmul_mx(
-                        out=banks[i][g][:, t % 2, :],
-                        lhsT=w_codes[:, t, :].bitcast(E2M1X4),
-                        lhsT_scale=w_plane[:, t, :],
-                        rhs=x_codes[:, i, :].bitcast(E4M3X4),
-                        rhs_scale=x_scales[:, i, :],
-                        start=True,
-                        stop=True,
-                    )
+                first_pass(high_banks[t - 2][:, i, :], t, x_codes[i][:], x_scales[i][:])
 
         entry = sb("entry", [P, PACK, J], F32)
         d_entry = sb("d_entry", [P, PACK, J], F32)
-        hid_slabs = sb("hid_slabs", [P, PACK, J], F32)
-        token_term = sb("token_term", [P, PACK, J], F32)
+        by_entry = sb("by_entry", [P, PACK, 2, J], F32)
         entry_term = sb("entry_term", [P, PACK, J], F32)
-        for g in range(2):
-            pair = slice(2 * g, 2 * g + 2)
-            for t in (2 * g, 2 * g + 1):
-                if t == 1:
-                    nc.vector.tensor_copy(entry[:, t, :], tb_rows[g][:, t % 2, :].indirect(lists[2][:]))
-                else:
-                    nc.scalar.activation(entry[:, t, :], tb_rows[g][:, t % 2, :].indirect(lists[2][:]), COPY)
-            for t in (2 * g, 2 * g + 1):
-                nc.scalar.activation(d_entry[:, t, :], tb_rows[g][:, t % 2, :].indirect(lists[3][:]), COPY)
-            nc.vector.tensor_tensor(out=hid_slabs[:, pair, :], in0=banks[0][g][:], in1=entry[:, pair, :], op=MULT)
-            nc.vector.scalar_tensor_tensor(
-                out=token_term[:, pair, :], in0=banks[1][g][:], scalar=0.5, in1=entry[:, pair, :], op0=MULT, op1=MULT
-            )
-            nc.vector.scalar_tensor_tensor(
-                out=entry_term[:, pair, :], in0=banks[0][g][:], scalar=0.5, in1=d_entry[:, pair, :], op0=MULT, op1=MULT
-            )
+
+        def half_product(product, sums, factors):
+            nc.vector.scalar_tensor_tensor(out=product, in0=sums, scalar=0.5, in1=factors, op0=MULT, op1=MULT)
+
+        nc.scalar.activation(entry[:, 0, :], tb_rows[0].indirect(lists[2][:]), COPY)
+        nc.vector.tensor_copy(entry[:, 1, :], tb_rows[1].indirect(lists[2][:]))
+        for t in (0, 1):
+            nc.scalar.activation(d_entry[:, t, :], tb_rows[t].indirect(lists[3][:]), COPY)
+        for i in range(2):
+            half_product(by_entry[:, 0:2, i, :], low_banks[i][:], entry[:, 0:2, :])
+        half_product(entry_term[:, 0:2, :], low_banks[0][:], d_entry[:, 0:2, :])
+        for t in (2, 3):
+            nc.scalar.activation(entry[:, t, :], tb_rows[t].indirect(lists[2][:]), COPY)
+            nc.scalar.activation(d_entry[:, t, :], tb_rows[t].indirect(lists[3][:]), COPY)
+            half_product(by_entry[:, t, :, :], high_banks[t - 2][:], entry[:, t : t + 1, :].to_broadcast([P, 2, J]))
+            half_product(entry_term[:, t, :], high_banks[t - 2][:, 0, :], d_entry[:, t, :])
 
         halves = [slice(h * JH, (h + 1) * JH) for h in range(HALVES)]
-        hid = sb("hid", [P, J, PACK], BF16)
-        hid_codes = sb("hid_codes", [P, J], U32)
-        hid_scales = sb("hid_scales", [P, J], U8)
+        hid = [sb("hid%d" % h, [P, JH, PACK], BF16) for h in range(HALVES)]
+        hid_codes = [sb("hid_codes%d" % h, [P, JH], U32) for h in range(HALVES)]
+        hid_scales = [sb("hid_scales%d" % h, [P, JH], U8) for h in range(HALVES)]
         dh = [sb("dh%d" % h, [P, JH, PACK], BF16) for h in range(HALVES)]
         dh_codes = [sb("dh_codes%d" % h, [P, JH], U32) for h in range(HALVES)]
         dh_scales = [sb("dh_scales%d" % h, [P, JH], U8) for h in range(HALVES)]
@@ -141,21 +152,22 @@ def tile_list_firstorder_two_moved_kernel(
         def join_terms(h):
             nc.vector.tensor_tensor(
                 out=woven_by_runs(dh[h][:]),
-                in0=by_runs(token_term[:, :, halves[h]]),
+                in0=by_runs(by_entry[:, :, 1, halves[h]]),
                 in1=by_runs(entry_term[:, :, halves[h]]),
                 op=ADD,
             )
 
-        nc.scalar.copy(out=woven_by_runs(hid[:]), in_=by_runs(hid_slabs[:]))
-        join_terms(0)
-        nc.vector.quantize_mx(
-            out=hid_codes[:].bitcast(E4M3X4), scales=hid_scales[:], in_=hid[:].rearrange("p j t -> p (j t)")
-        )
-        join_terms(1)
+        def quantize(codes, scales, woven, fmt):
+            nc.vector.quantize_mx(out=codes[:].bitcast(fmt), scales=scales[:], in_=woven[:].rearrange("p j t -> p (j t)"))
+
         for h in range(HALVES):
-            nc.vector.quantize_mx(
-                out=dh_codes[h][:].bitcast(E5M2X4), scales=dh_scales[h][:], in_=dh[h][:].rearrange("p j t -> p (j t)")
-            )
+            nc.scalar.activation(woven_by_runs(hid[h][:]), by_runs(by_entry[:, :, 0, halves[h]]), COPY, scale=2.0)
+        join_terms(0)
+        quantize(hid_codes[0], hid_scales[0], hid[0], E4M3X4)
+        join_terms(1)
+        quantize(hid_codes[1], hid_scales[1], hid[1], E4M3X4)
+        quantize(dh_codes[0], dh_scales[0], dh[0], E5M2X4)
+        quantize(dh_codes[1], dh_scales[1], dh[1], E5M2X4)
 
         out_rows = out.rearrange("(u p) j -> p u j", p=P)
         out_banks = [[psum.tile([P, JH], F32, name="out_bank%d_%d" % (h, u)) for u in range(N // P)] for h in range(HALVES)]
@@ -174,7 +186,7 @@ def tile_list_firstorder_two_moved_kernel(
 
         for h in range(HALVES):
             for u in range(N // P):
-                second_pass(h, u, hid_codes[:, halves[h]].bitcast(E4M3X4), hid_scales[:, halves[h]], True)
+                second_pass(h, u, hid_codes[h][:].bitcast(E4M3X4), hid_scales[h][:], True)
         for h in range(HALVES):
             result = sb("result%d" % h, [P, N // P, JH], F32)
             for u in range(N // P):

from contextlib import ExitStack

import concourse.mybir as mybir

K, T, J, R, V, N = 512, 2048, 256, 512, 512, 256
FLOPS = 2 * (2 * K * R * J + 2 * R * N * J)

F32 = mybir.dt.float32
BF16 = mybir.dt.bfloat16
I32 = mybir.dt.int32
U32 = mybir.dt.uint32
U16 = mybir.dt.uint16
U8 = mybir.dt.uint8
E4M3X4 = mybir.dt.float8_e4m3fn_x4
E5M2X4 = mybir.dt.float8_e5m2_x4
E2M1X4 = mybir.dt.float4_e2m1fn_x4
MULT = mybir.AluOpType.mult
ADD = mybir.AluOpType.add
COPY = mybir.ActivationFunctionType.Copy

P = 128
PACK = 4
HALVES = 2
JH = J // HALVES
RUN = 4


def load_scale_rows(queues, plane, scales):
    for q, queue in enumerate(queues):
        queue.dma_start(out=plane[32 * q : 32 * q + 4, :].bitcast(I32), in_=scales[0, 4 * q : 4 * q + 4, :].bitcast(I32))


def by_runs(slabs):
    return slabs.rearrange("p t (c i) -> p c t i", i=RUN)


def woven_by_runs(woven):
    return woven.rearrange("p (c i) t -> p c t i", i=RUN)


def tile_list_firstorder_two_moved_kernel(
    tc, xt_words, xt_scales, w_words, w_scales, tb, wb_words, wb_scales, offs, offs2, offs3, offs4, out
):
    nc = tc.nc
    with ExitStack() as ctx:
        keep = ctx.enter_context(tc.tile_pool(name="keep", bufs=1))
        psum = ctx.enter_context(tc.psum_pool(name="psum", bufs=1))

        def sb(name, shape, dtype, tag=None):
            return keep.tile(shape, dtype, name=name, tag=tag or name, align_bytes=64)

        lists = [keep.tile([P, J // 16], U16, name="list%d" % i) for i in range(4)]
        x_table = sb("x_table", [P, T], I32)
        x_plane = sb("x_plane", [P, T], U8, tag="x_plane_then_wb")
        w_raw = sb("w_raw", [P, 2 * R], U8)
        w_raw_plane = sb("w_raw_plane", [P, R], U8, tag="w_plane_then_codes")
        wb_plane = sb("wb_plane", [P, N], U8)
        tb_low = sb("tb_low", [P, 2, V], F32)
        tb_high = [sb("tb_high%d" % t, [P, V], F32) for t in range(2)]
        tb_rows = [tb_low[:, 0, :], tb_low[:, 1, :], tb_high[0][:], tb_high[1][:]]

        nc.vector.memset(x_plane[:, : T // 2].bitcast(I32), 0)
        nc.gpsimd.memset(x_plane[:, T // 2 :].bitcast(I32), 0)
        nc.vector.memset(w_raw_plane[:].bitcast(I32), 0)
        nc.vector.memset(wb_plane[:].bitcast(I32), 0)

        warm = sb("warm", [P, 16], F32)
        nc.vector.memset(warm[:, 0:1], 0.0)

        tb_dealt = tb.rearrange("(p t) v -> p t v", t=PACK)
        nc.sync.dma_start(lists[0][:], offs)
        nc.sync.dma_start(lists[1][:], offs2)
        nc.sync.dma_start(out=w_raw[:].bitcast(I32), in_=w_words[0].bitcast(I32))
        load_scale_rows([nc.sync, nc.scalar] * 2, x_plane, xt_scales)
        nc.sync.dma_start(out=x_table[:], in_=xt_words[0].rearrange("p n t -> p (n t)").bitcast(I32))
        load_scale_rows([nc.sync] * 4, w_raw_plane, w_scales)
        nc.sync.dma_start(out=tb_low[:], in_=tb_dealt[:, 0:2, :])
        nc.sync.dma_start(lists[2][:], offs3)
        nc.sync.dma_start(lists[3][:], offs4)
        for t in (2, 3):
            nc.sync.dma_start(out=tb_rows[t], in_=tb_dealt[:, t, :])

        nc.scalar.activation(warm[:, 8:9], warm[:, 0:1], COPY)

        w_codes = sb("w_codes", [P, PACK, 2 * P], U8)
        w_plane = sb("w_plane", [P, PACK, P], U8)
        nc.vector.tensor_copy(out=w_codes[:].bitcast(U16), in_=w_raw[:].bitcast(U16).rearrange("p (m t) -> p t m", t=PACK))

        x_scales = [sb("x_scales%d" % i, [P, J], U8) for i in range(2)]
        for i in range(2):
            nc.vector.tensor_copy(x_scales[i][:], x_plane[:].indirect(lists[i][:]))
        token_codes = sb("token_codes", [P, J], U32)
        nc.vector.tensor_copy(token_codes[:], x_table[:].bitcast(U32).indirect(lists[0][:]))
        nc.vector.tensor_copy(out=w_plane[:], in_=w_raw_plane[:].rearrange("p (m t) -> p t m", t=PACK))
        change_codes = sb("change_codes", [P, J], U32, tag="w_plane_then_codes")
        nc.vector.tensor_copy(change_codes[:], x_table[:].bitcast(U32).indirect(lists[1][:]))
        x_codes = [token_codes, change_codes]

        wb_codes = sb("wb_codes", [P, N], I32, tag="x_plane_then_wb")
        nc.sync.dma_start(out=wb_codes[:], in_=wb_words[0].rearrange("p n t -> p (n t)").bitcast(I32))
        load_scale_rows([nc.sync] * 4, wb_plane, wb_scales)

        def first_pass(bank_cols, t, codes, scales):
            nc.tensor.matmul_mx(
                out=bank_cols,
                lhsT=w_codes[:, t, :].bitcast(E2M1X4),
                lhsT_scale=w_plane[:, t, :],
                rhs=codes.bitcast(E4M3X4),
                rhs_scale=scales,
                start=True,
                stop=True,
            )

        low_banks = [psum.tile([P, 2, J], F32, name="low_bank%d" % i) for i in range(2)]
        high_banks = [psum.tile([P, 2, J], F32, name="high_bank%d" % t) for t in range(2)]
        for i in range(2):
            for t in (0, 1):
                first_pass(low_banks[i][:, t, :], t, x_codes[i][:], x_scales[i][:])
        for t in (2, 3):
            for i in range(2):
                first_pass(high_banks[t - 2][:, i, :], t, x_codes[i][:], x_scales[i][:])

        entry = sb("entry", [P, PACK, J], F32)
        d_entry = sb("d_entry", [P, PACK, J], F32)
        by_entry = sb("by_entry", [P, PACK, 2, J], F32)
        entry_term = sb("entry_term", [P, PACK, J], F32)

        def half_product(product, sums, factors):
            nc.vector.scalar_tensor_tensor(out=product, in0=sums, scalar=0.5, in1=factors, op0=MULT, op1=MULT)

        nc.scalar.activation(entry[:, 0, :], tb_rows[0].indirect(lists[2][:]), COPY)
        nc.vector.tensor_copy(entry[:, 1, :], tb_rows[1].indirect(lists[2][:]))
        for t in (0, 1):
            nc.scalar.activation(d_entry[:, t, :], tb_rows[t].indirect(lists[3][:]), COPY)
        for i in range(2):
            half_product(by_entry[:, 0:2, i, :], low_banks[i][:], entry[:, 0:2, :])
        half_product(entry_term[:, 0:2, :], low_banks[0][:], d_entry[:, 0:2, :])
        for t in (2, 3):
            nc.scalar.activation(entry[:, t, :], tb_rows[t].indirect(lists[2][:]), COPY)
            nc.scalar.activation(d_entry[:, t, :], tb_rows[t].indirect(lists[3][:]), COPY)
            half_product(by_entry[:, t, :, :], high_banks[t - 2][:], entry[:, t : t + 1, :].to_broadcast([P, 2, J]))
            half_product(entry_term[:, t, :], high_banks[t - 2][:, 0, :], d_entry[:, t, :])

        halves = [slice(h * JH, (h + 1) * JH) for h in range(HALVES)]
        hid = [sb("hid%d" % h, [P, JH, PACK], BF16) for h in range(HALVES)]
        hid_codes = [sb("hid_codes%d" % h, [P, JH], U32) for h in range(HALVES)]
        hid_scales = [sb("hid_scales%d" % h, [P, JH], U8) for h in range(HALVES)]
        dh = [sb("dh%d" % h, [P, JH, PACK], BF16) for h in range(HALVES)]
        dh_codes = [sb("dh_codes%d" % h, [P, JH], U32) for h in range(HALVES)]
        dh_scales = [sb("dh_scales%d" % h, [P, JH], U8) for h in range(HALVES)]

        def join_terms(h):
            nc.vector.tensor_tensor(
                out=woven_by_runs(dh[h][:]),
                in0=by_runs(by_entry[:, :, 1, halves[h]]),
                in1=by_runs(entry_term[:, :, halves[h]]),
                op=ADD,
            )

        def quantize(codes, scales, woven, fmt):
            nc.vector.quantize_mx(out=codes[:].bitcast(fmt), scales=scales[:], in_=woven[:].rearrange("p j t -> p (j t)"))

        for h in range(HALVES):
            nc.scalar.activation(woven_by_runs(hid[h][:]), by_runs(by_entry[:, :, 0, halves[h]]), COPY, scale=2.0)
        join_terms(0)
        quantize(hid_codes[0], hid_scales[0], hid[0], E4M3X4)
        join_terms(1)
        quantize(hid_codes[1], hid_scales[1], hid[1], E4M3X4)
        quantize(dh_codes[0], dh_scales[0], dh[0], E5M2X4)
        quantize(dh_codes[1], dh_scales[1], dh[1], E5M2X4)

        out_rows = out.rearrange("(u p) j -> p u j", p=P)
        out_banks = [[psum.tile([P, JH], F32, name="out_bank%d_%d" % (h, u)) for u in range(N // P)] for h in range(HALVES)]

        def second_pass(h, u, codes, scales, first):
            feats = slice(u * P, (u + 1) * P)
            nc.tensor.matmul_mx(
                out=out_banks[h][u][:],
                lhsT=wb_codes[:, feats].bitcast(E5M2X4),
                lhsT_scale=wb_plane[:, feats],
                rhs=codes,
                rhs_scale=scales,
                start=first,
                stop=not first,
            )

        for h in range(HALVES):
            for u in range(N // P):
                second_pass(h, u, hid_codes[h][:].bitcast(E4M3X4), hid_scales[h][:], True)
        for h in range(HALVES):
            result = sb("result%d" % h, [P, N // P, JH], F32)
            for u in range(N // P):
                second_pass(h, u, dh_codes[h][:].bitcast(E5M2X4), dh_scales[h][:], False)
                if u == 1:
                    nc.vector.tensor_copy(out=result[:, u, :], in_=out_banks[h][u][:])
                else:
                    nc.scalar.copy(out=result[:, u, :], in_=out_banks[h][u][:])
            nc.sync.dma_start(out=out_rows[:, :, halves[h]], in_=result[:])
